import numpy as np
import ml_dtypes


def mxq(x, axis, fmt="e4m3"):
    dtype, down = {"e4m3": (ml_dtypes.float8_e4m3fn, 7), "e5m2": (ml_dtypes.float8_e5m2, 14)}[fmt]
    v = np.moveaxis(np.asarray(x, np.float32).astype(ml_dtypes.bfloat16).astype(np.float64), axis, -1)
    blocks = v.reshape(v.shape[:-1] + (-1, 32))
    amax = np.abs(blocks).max(-1, keepdims=True)
    byte = np.maximum(np.where(amax > 0, np.frexp(amax)[1] - 1 + 127, 0) - down, 1)
    scale = np.exp2(byte - 127.0)
    codes = (blocks / scale).astype(np.float32).astype(dtype).astype(np.float64)
    return np.moveaxis((codes * scale).reshape(v.shape), -1, axis)


WIDE = False


def mx_kscale(k):
    if not WIDE:
        return np.ones(k)
    levels = np.array([10, -10, 5, -5, 0])
    if k % 512:
        return np.exp2(np.random.permutation(np.resize(levels, k // 32))).repeat(32)
    a = np.empty((k // 512, 16))
    for p in range(k // 512):
        a[p, :8] = np.random.permutation(np.resize(levels, 8))
        for g in range(8):
            far = levels[np.abs(levels - a[p, g]) >= 10]
            a[p, g + 8] = far[np.random.randint(len(far))]
    return np.exp2(a.ravel()).repeat(32)


def f64(x):
    return np.asarray(x).astype(np.float64)


def striped(idx):
    return np.tile(idx.reshape(-1, 16).T, (8, 1)).astype(np.uint16)


def unstriped(offs):
    return offs[:16].T.reshape(-1).astype(np.int64)


def striped8(idx):
    return np.concatenate([x.reshape(-1, 16).T for x in idx]).astype(np.uint16)


def runs(offs, k):
    lists = np.stack([offs[16 * r : 16 * r + 16].T.reshape(-1) for r in range(8)]).astype(np.int64)
    return lists[np.arange(k) % 512 // 64]


def pack_weight(w):
    k, n = w.shape
    w = f64(np.asarray(w, np.float32).astype(ml_dtypes.bfloat16)).reshape(k // 32, 32, n)
    amax = np.abs(w).max(1)
    byte = np.clip(np.where(amax > 0, np.frexp(amax)[1] - 1 + 127 - 7, 1), 1, 254)
    scaled = (w * np.exp2(127.0 - byte)[:, None, :]).reshape(k, n).astype(np.float32)
    words = np.ascontiguousarray(scaled.reshape(k // 512, 128, 4, n).transpose(0, 1, 3, 2)).astype(ml_dtypes.float8_e4m3fn).view(np.uint8)
    return words, np.ascontiguousarray(byte.astype(np.uint8).reshape(k // 512, 16, n))


def unpack_weight(words, scales):
    g, p, n, _ = words.shape
    vals = np.ascontiguousarray(words).view(ml_dtypes.float8_e4m3fn).astype(np.float64) * np.repeat(np.exp2(scales.astype(np.float64) - 127.0), 8, axis=1)[..., None]
    return vals.transpose(0, 1, 3, 2).reshape(g * 512, n)


K, T, S, H, W, G = 512, 1024, 256, 512, 128, 2048


def setup_inputs():
    n = np.random.standard_normal
    s = mx_kscale(K)[:, None]
    packed_xT = pack_weight(n((K, T)) * s)
    packed_dT = pack_weight(n((K, G)) / s)
    perm = np.random.permutation(S)
    return {
        "x_words": packed_xT[0],
        "x_scales": packed_xT[1],
        "w1": (n((K, H)) / np.sqrt(2 * K) / s).astype(np.float32),
        "w2": (n((K, H)) / np.sqrt(2 * K) / s).astype(np.float32),
        "gs": (np.random.uniform(0.5, 1.5, (K, 1)) * s).astype(np.float32),
        "d_words": packed_dT[0],
        "d_scales": packed_dT[1],
        "offs": striped8(np.random.randint(0, T, (8, S))),
        "hz": striped8(np.random.randint(0, T, (8, S))),
        "n1": striped(perm[:W]),
        "n2": striped(perm[W:]),
        "k1": striped8(np.random.randint(0, G, (8, H))),
        "n3": striped(np.random.permutation(S)),
        "n4": striped(np.random.permutation(S)),
    }


def reference(x_words, x_scales, w1, w2, gs, d_words, d_scales, offs, hz, n1, n2, k1, n3, n4):
    d_k1 = unpack_weight(d_words, d_scales)[np.arange(K)[:, None], runs(k1, K)]
    xq = unpack_weight(x_words, x_scales)[np.arange(K)[:, None], runs(offs, K)]
    x_hz = unpack_weight(x_words, x_scales)[np.arange(K)[:, None], runs(hz, K)]
    y = mxq(f64(w1), 0, "e4m3").T @ xq + mxq(f64(w2), 0, "e4m3").T @ x_hz
    pa = y[:, unstriped(n1)]
    pb = y[:, unstriped(n2)]
    ra = np.maximum(pa, pb)
    ds = y.copy()
    ds[:, unstriped(n1)] = ra
    z = f64(gs) * ds
    h = 0.0625 * ((d_k1.T @ mxq(z, 0, "e4m3")))
    ds2 = np.zeros((H, S))
    ds2[:, unstriped(n3)] = h
    ds3 = np.zeros((H, S))
    ds3[:, unstriped(n4)] = h
    return np.maximum(ds2, ds3)

@@ -1,0 +1,213 @@
+from contextlib import ExitStack
+
+import concourse.mybir as mybir
+
+K, T, S, H, W, G = 512, 1024, 256, 512, 128, 2048
+FLOPS = 2 * K * H * S * 3
+
+F32 = mybir.dt.float32
+BF16 = mybir.dt.bfloat16
+I32 = mybir.dt.int32
+U32 = mybir.dt.uint32
+U16 = mybir.dt.uint16
+U8 = mybir.dt.uint8
+FP8X4 = mybir.dt.float8_e4m3fn_x4
+COPY = mybir.ActivationFunctionType.Copy
+MULT = mybir.AluOpType.mult
+MAX = mybir.AluOpType.max
+
+P = 128
+PACK = 4
+
+
+def tile_picked_dhqfillsendtwo_none_p_kernel(
+    tc, x_words, x_scales, w1, w2, gs, d_words, d_scales, offs, hz, n1, n2, k1, n3, n4, out
+):
+    nc = tc.nc
+    with ExitStack() as ctx:
+        lists = ctx.enter_context(tc.tile_pool(name="lists", bufs=1))
+        keep = ctx.enter_context(tc.tile_pool(name="keep", bufs=1))
+        psum = ctx.enter_context(tc.psum_pool(name="psum", bufs=1))
+
+        def load_list(src, name):
+            tile = lists.tile(list(src.shape), U16, name=name)
+            nc.sync.dma_start(tile[:], src)
+            return tile
+
+        def load_scale_rows(queue, table, scales):
+            rows = scales[0].bitcast(I32)
+            words = rows.shape[1]
+            for r in range(2):
+                queue.dma_start(
+                    table[r:P:2, :].bitcast(I32), rows[r:16:2, :].unsqueeze(1).to_broadcast([8, 8, words])
+                )
+
+        def place_scale_rows(queue, plane, picked):
+            nc.vector.tensor_copy(plane[:].bitcast(I32), picked[:].bitcast(I32))
+            for r in range(2):
+                queue.dma_start(plane[2 + r : P : 32, :].bitcast(I32), picked[16 + r : P : 32, :].bitcast(I32))
+
+        def scalar_round(dst, src):
+            nc.scalar.activation(dst, src, COPY)
+
+        def round_weight(engine_copy, grouped, raw, raw_m0, m0, m1):
+            src = raw[:].rearrange("p j (m t) -> p m j t", t=PACK)
+            dst = grouped[:].rearrange("p (t m j) -> p m j t", t=PACK, j=PACK)
+            engine_copy(dst[:, m0:m1], src[:, m0 - raw_m0 : m1 - raw_m0])
+
+        x_scale_table = keep.tile([P, T], U8, name="x_scale_table", tag="scale_table")
+
+        offs_l = load_list(offs, "offs_l")
+        hz_l = load_list(hz, "hz_l")
+        load_scale_rows(nc.sync, x_scale_table, x_scales)
+
+        x_table = keep.tile([P, T], U32, name="x_table")
+        nc.scalar.dma_start(x_table[:].bitcast(I32), x_words[0].rearrange("p n t -> p (n t)").bitcast(I32))
+        k1_l = load_list(k1, "k1_l")
+        n1_l = load_list(n1, "n1_l")
+        w1_raw = keep.tile([P, PACK, H], F32, name="w1_raw")
+        nc.sync.dma_start(w1_raw[:], w1.rearrange("(p j) c -> p j c", j=PACK))
+        w2_rows = w2.rearrange("(p j) c -> p j c", j=PACK)
+        w2_head = keep.tile([P, PACK, 384], F32, name="w2_head", tag="shared")
+        nc.sync.dma_start(w2_head[:], w2_rows[:, :, 0:384])
+        w2_tail = keep.tile([P, PACK, 128], F32, name="w2_tail")
+        nc.sync.dma_start(w2_tail[:], w2_rows[:, :, 384:512])
+
+        n2_l = load_list(n2, "n2_l")
+        n3_l = load_list(n3, "n3_l")
+        n4_l = load_list(n4, "n4_l")
+        gain = keep.tile([P, PACK], F32, name="gain")
+        nc.gpsimd.dma_start(gain[:], gs.rearrange("(p t) o -> p (t o)", t=PACK))
+
+        x_scale_picked = keep.tile([P, 2 * S], U8, name="x_scale_picked")
+        nc.vector.tensor_copy(x_scale_picked[:, 0:S], x_scale_table[:].indirect(offs_l[:]))
+        nc.vector.tensor_copy(x_scale_picked[:, S : 2 * S], x_scale_table[:].indirect(hz_l[:]))
+        x_plane = keep.tile([P, 2 * S], U8, name="x_plane", align_bytes=64)
+        place_scale_rows(nc.scalar, x_plane, x_scale_picked)
+
+        x_a = keep.tile([P, S], U32, name="x_a", align_bytes=64)
+        x_b = keep.tile([P, S], U32, name="x_b", align_bytes=64)
+        nc.vector.tensor_copy(x_a[:], x_table[:].indirect(offs_l[:]))
+        nc.vector.tensor_copy(x_b[:], x_table[:].indirect(hz_l[:]))
+
+        d_scale_table = keep.tile([P, G], U8, name="d_scale_table", tag="scale_table")
+        load_scale_rows(nc.sync, d_scale_table, d_scales)
+
+        w1_bf = keep.tile([P, PACK * H], BF16, name="w1_bf", align_bytes=64)
+        w2_bf = keep.tile([P, PACK * H], BF16, name="w2_bf", align_bytes=64)
+        round_weight(scalar_round, w1_bf, w1_raw, 0, 0, 32)
+        round_weight(nc.vector.tensor_copy, w1_bf, w1_raw, 0, 32, 128)
+
+        w1_codes = keep.tile([P, H], U32, name="w1_codes", align_bytes=64)
+        w1_plane = keep.tile([P, H], U8, name="w1_plane", align_bytes=64)
+        nc.vector.quantize_mx(w1_codes[:].bitcast(FP8X4), w1_plane[:], w1_bf[:])
+
+        round_weight(nc.vector.tensor_copy, w2_bf, w2_head, 0, 0, 64)
+        round_weight(scalar_round, w2_bf, w2_head, 0, 64, 96)
+        round_weight(nc.vector.tensor_copy, w2_bf, w2_tail, 96, 96, 128)
+
+        d_table = keep.tile([P, G], U32, name="d_table", tag="shared")
+        nc.sync.dma_start(d_table[:].bitcast(I32), d_words[0].rearrange("p n t -> p (n t)").bitcast(I32))
+
+        w2_codes = keep.tile([P, H], U32, name="w2_codes", align_bytes=64)
+        w2_plane = keep.tile([P, H], U8, name="w2_plane", align_bytes=64)
+        y_banks = [psum.tile([P, S], F32, name=f"y_bank{t}", tag=f"bank{t}") for t in range(PACK)]
+        for t in range(PACK):
+            cols = slice(P * t, P * (t + 1))
+            nc.tensor.matmul_mx(
+                y_banks[t][:], lhsT=w1_codes[:, cols].bitcast(FP8X4), lhsT_scale=w1_plane[:, cols],
+                rhs=x_a[:].bitcast(FP8X4), rhs_scale=x_plane[:, 0:S], start=True, stop=False,
+            )
+        for t in range(PACK):
+            cols = slice(P * t, P * (t + 1))
+            nc.vector.quantize_mx(
+                w2_codes[:, cols].bitcast(FP8X4), w2_plane[:, cols], w2_bf[:, H * t : H * (t + 1)]
+            )
+            nc.tensor.matmul_mx(
+                y_banks[t][:], lhsT=w2_codes[:, cols].bitcast(FP8X4), lhsT_scale=w2_plane[:, cols],
+                rhs=x_b[:].bitcast(FP8X4), rhs_scale=x_plane[:, S : 2 * S], start=False, stop=True,
+            )
+
+        d_codes = keep.tile([P, H], U32, name="d_codes", align_bytes=64)
+        z_bf = [keep.tile([P, W, PACK], BF16, name=f"z_bf{u}", align_bytes=64) for u in range(2)]
+        ys, larger = [], []
+
+        def fetch_pairs(t):
+            y = keep.tile([P, S], F32, name=f"y{t}")
+            if t == 0:
+                nc.scalar.copy(y[:], y_banks[t][:])
+            else:
+                nc.vector.tensor_copy(y[:], y_banks[t][:])
+            pa = keep.tile([P, W], F32, name=f"pa{t}")
+            pb = keep.tile([P, W], F32, name=f"pb{t}")
+            nc.scalar.activation(pa[:], y[:].indirect(n1_l[:]), COPY)
+            nc.scalar.activation(pb[:], y[:].indirect(n2_l[:]), COPY)
+            ra = keep.tile([P, W], F32, name=f"ra{t}")
+            nc.vector.tensor_tensor(ra[:], pa[:], pb[:], MAX)
+            ys.append(y)
+            larger.append(ra)
+
+        def put_back(t):
+            nc.scalar.activation(ys[t][:].indirect(n1_l[:]), larger[t][:], COPY)
+            for u in range(2):
+                nc.vector.tensor_scalar(
+                    z_bf[u][:, :, t], ys[t][:, W * u : W * (u + 1)], gain[:, t : t + 1], None, MULT
+                )
+
+        fetch_pairs(0)
+        d_scale_picked = keep.tile([P, H], U8, name="d_scale_picked")
+        nc.vector.tensor_copy(d_scale_picked[:], d_scale_table[:].indirect(k1_l[:]))
+        d_plane = keep.tile([P, H], U8, name="d_plane", align_bytes=64)
+        place_scale_rows(nc.sync, d_plane, d_scale_picked)
+        for t in range(1, PACK):
+            fetch_pairs(t)
+            put_back(t - 1)
+            if t < 3:
+                half = slice(S * (t - 1), S * t)
+                nc.vector.tensor_copy(d_codes[:, half], d_table[:].indirect(k1_l[:, 16 * (t - 1) : 16 * t]))
+        put_back(PACK - 1)
+
+        z_codes = keep.tile([P, S], U32, name="z_codes", align_bytes=64)
+        z_plane = keep.tile([P, S], U8, name="z_plane", align_bytes=64)
+        for u in range(2):
+            cols = slice(W * u, W * (u + 1))
+            nc.vector.quantize_mx(
+                z_codes[:, cols].bitcast(FP8X4), z_plane[:, cols], z_bf[u][:].rearrange("p c t -> p (c t)")
+            )
+
+        def product(bank, m, cols):
+            rows = slice(P * m, P * (m + 1))
+            nc.tensor.matmul_mx(
+                bank[:], lhsT=d_codes[:, rows].bitcast(FP8X4), lhsT_scale=d_plane[:, rows],
+                rhs=z_codes[:, cols].bitcast(FP8X4), rhs_scale=z_plane[:, cols], start=True, stop=True,
+            )
+
+        def finish(m, sent3, sent4):
+            res = keep.tile([P, S], F32, name=f"res{m}")
+            nc.vector.tensor_tensor(res[:], sent3[:, 0:S], sent4[:, 0:S], MAX)
+            nc.sync.dma_start(out[P * m : P * (m + 1), :], res[:])
+
+        sent3 = keep.tile([P, S], F32, name="sent3_0")
+        sent4 = keep.tile([P, S], F32, name="sent4_0")
+        for u in range(2):
+            bank = psum.tile([P, W], F32, name=f"h_bank0_{u}", tag=f"bank{4 + u}")
+            product(bank, 0, slice(W * u, W * (u + 1)))
+            h = keep.tile([P, W], F32, name=f"h0_{u}")
+            if u == 0:
+                nc.scalar.activation(h[:], bank[:], COPY, scale=0.0625)
+            else:
+                nc.vector.tensor_scalar(h[:], bank[:], 0.0625, None, MULT)
+            nc.scalar.activation(sent3[:].indirect(n3_l[:, 8 * u : 8 * (u + 1)]), h[:], COPY)
+            nc.scalar.activation(sent4[:].indirect(n4_l[:, 8 * u : 8 * (u + 1)]), h[:], COPY)
+        finish(0, sent3, sent4)
+
+        for m in range(1, PACK):
+            bank = psum.tile([P, S], F32, name=f"h_bank{m}", tag=f"bank{(5 + m) % 8}")
+            product(bank, m, slice(0, S))
+            h = keep.tile([P, S], F32, name=f"h{m}")
+            nc.vector.tensor_scalar(h[:], bank[:], 0.0625, None, MULT)
+            sent3 = keep.tile([P, 2 * S], F32, name=f"sent3_{m}")
+            sent4 = keep.tile([P, 2 * S], F32, name=f"sent4_{m}")
+            nc.scalar.activation(sent3[:].indirect(n3_l[:]), h[:], COPY)
+            nc.scalar.activation(sent4[:].indirect(n4_l[:]), h[:], COPY)
+            finish(m, sent3, sent4)

@@ -55,7 +55,7 @@ def tile_picked_dhqfillsendtwo_none_p_kernel(
             dst = grouped[:].rearrange("p (t m j) -> p m j t", t=PACK, j=PACK)
             engine_copy(dst[:, m0:m1], src[:, m0 - raw_m0 : m1 - raw_m0])
 
-        x_scale_table = keep.tile([P, T], U8, name="x_scale_table", tag="scale_table")
+        x_scale_table = keep.tile([P, T], U8, name="x_scale_table")
 
         offs_l = load_list(offs, "offs_l")
         hz_l = load_list(hz, "hz_l")
@@ -65,10 +65,10 @@ def tile_picked_dhqfillsendtwo_none_p_kernel(
         nc.scalar.dma_start(x_table[:].bitcast(I32), x_words[0].rearrange("p n t -> p (n t)").bitcast(I32))
         k1_l = load_list(k1, "k1_l")
         n1_l = load_list(n1, "n1_l")
-        w1_raw = keep.tile([P, PACK, H], F32, name="w1_raw")
+        w1_raw = keep.tile([P, PACK, H], F32, name="w1_raw", tag="wide")
         nc.sync.dma_start(w1_raw[:], w1.rearrange("(p j) c -> p j c", j=PACK))
         w2_rows = w2.rearrange("(p j) c -> p j c", j=PACK)
-        w2_head = keep.tile([P, PACK, 384], F32, name="w2_head", tag="shared")
+        w2_head = keep.tile([P, PACK, 384], F32, name="w2_head")
         nc.sync.dma_start(w2_head[:], w2_rows[:, :, 0:384])
         w2_tail = keep.tile([P, PACK, 128], F32, name="w2_tail")
         nc.sync.dma_start(w2_tail[:], w2_rows[:, :, 384:512])
@@ -76,6 +76,10 @@ def tile_picked_dhqfillsendtwo_none_p_kernel(
         n2_l = load_list(n2, "n2_l")
         n3_l = load_list(n3, "n3_l")
         n4_l = load_list(n4, "n4_l")
+        d_scale_table = keep.tile([P, G], U8, name="d_scale_table")
+        nc.gpsimd.memset(d_scale_table[:].bitcast(I32), 0)
+        for r in range(2):
+            nc.gpsimd.dma_start(d_scale_table[r:P:16, :].bitcast(I32), d_scales[0].bitcast(I32)[r:16:2, :])
         gain = keep.tile([P, PACK], F32, name="gain")
         nc.gpsimd.dma_start(gain[:], gs.rearrange("(p t) o -> p (t o)", t=PACK))
 
@@ -90,24 +94,22 @@ def tile_picked_dhqfillsendtwo_none_p_kernel(
         nc.vector.tensor_copy(x_a[:], x_table[:].indirect(offs_l[:]))
         nc.vector.tensor_copy(x_b[:], x_table[:].indirect(hz_l[:]))
 
-        d_scale_table = keep.tile([P, G], U8, name="d_scale_table", tag="scale_table")
-        load_scale_rows(nc.sync, d_scale_table, d_scales)
 
         w1_bf = keep.tile([P, PACK * H], BF16, name="w1_bf", align_bytes=64)
         w2_bf = keep.tile([P, PACK * H], BF16, name="w2_bf", align_bytes=64)
-        round_weight(scalar_round, w1_bf, w1_raw, 0, 0, 32)
-        round_weight(nc.vector.tensor_copy, w1_bf, w1_raw, 0, 32, 128)
+        round_weight(scalar_round, w1_bf, w1_raw, 0, 0, 56)
+        round_weight(nc.vector.tensor_copy, w1_bf, w1_raw, 0, 56, 128)
+
+        d_table = keep.tile([P, G], U32, name="d_table", tag="wide")
+        nc.sync.dma_start(d_table[:].bitcast(I32), d_words[0].rearrange("p n t -> p (n t)").bitcast(I32))
 
         w1_codes = keep.tile([P, H], U32, name="w1_codes", align_bytes=64)
         w1_plane = keep.tile([P, H], U8, name="w1_plane", align_bytes=64)
         nc.vector.quantize_mx(w1_codes[:].bitcast(FP8X4), w1_plane[:], w1_bf[:])
 
-        round_weight(nc.vector.tensor_copy, w2_bf, w2_head, 0, 0, 64)
-        round_weight(scalar_round, w2_bf, w2_head, 0, 64, 96)
+        round_weight(nc.vector.tensor_copy, w2_bf, w2_head, 0, 0, 48)
+        round_weight(scalar_round, w2_bf, w2_head, 0, 48, 96)
         round_weight(nc.vector.tensor_copy, w2_bf, w2_tail, 96, 96, 128)
-
-        d_table = keep.tile([P, G], U32, name="d_table", tag="shared")
-        nc.sync.dma_start(d_table[:].bitcast(I32), d_words[0].rearrange("p n t -> p (n t)").bitcast(I32))
 
         w2_codes = keep.tile([P, H], U32, name="w2_codes", align_bytes=64)
         w2_plane = keep.tile([P, H], U8, name="w2_plane", align_bytes=64)
@@ -128,7 +130,6 @@ def tile_picked_dhqfillsendtwo_none_p_kernel(
                 rhs=x_b[:].bitcast(FP8X4), rhs_scale=x_plane[:, S : 2 * S], start=False, stop=True,
             )
 
-        d_codes = keep.tile([P, H], U32, name="d_codes", align_bytes=64)
         z_bf = [keep.tile([P, W, PACK], BF16, name=f"z_bf{u}", align_bytes=64) for u in range(2)]
         ys, larger = [], []
 
@@ -138,11 +139,11 @@ def tile_picked_dhqfillsendtwo_none_p_kernel(
                 nc.scalar.copy(y[:], y_banks[t][:])
             else:
                 nc.vector.tensor_copy(y[:], y_banks[t][:])
-            pa = keep.tile([P, W], F32, name=f"pa{t}")
+            pa = keep.tile([P, W], F32, name=f"pa{t}", tag=f"pa{t}", align_bytes=64)
             pb = keep.tile([P, W], F32, name=f"pb{t}")
             nc.scalar.activation(pa[:], y[:].indirect(n1_l[:]), COPY)
             nc.scalar.activation(pb[:], y[:].indirect(n2_l[:]), COPY)
-            ra = keep.tile([P, W], F32, name=f"ra{t}")
+            ra = keep.tile([P, W], F32, name=f"ra{t}", tag="wide" if t == 3 else f"ra{t}")
             nc.vector.tensor_tensor(ra[:], pa[:], pb[:], MAX)
             ys.append(y)
             larger.append(ra)
@@ -155,17 +156,20 @@ def tile_picked_dhqfillsendtwo_none_p_kernel(
                 )
 
         fetch_pairs(0)
-        d_scale_picked = keep.tile([P, H], U8, name="d_scale_picked")
+        fetch_pairs(1)
+        d_scale_picked = keep.tile([P, H], U8, name="d_scale_picked", tag="pa0", align_bytes=64)
         nc.vector.tensor_copy(d_scale_picked[:], d_scale_table[:].indirect(k1_l[:]))
         d_plane = keep.tile([P, H], U8, name="d_plane", align_bytes=64)
         place_scale_rows(nc.sync, d_plane, d_scale_picked)
-        for t in range(1, PACK):
-            fetch_pairs(t)
-            put_back(t - 1)
-            if t < 3:
-                half = slice(S * (t - 1), S * t)
-                nc.vector.tensor_copy(d_codes[:, half], d_table[:].indirect(k1_l[:, 16 * (t - 1) : 16 * t]))
-        put_back(PACK - 1)
+        put_back(0)
+        fetch_pairs(2)
+        d_codes = keep.tile([P, H], U32, name="d_codes", align_bytes=64)
+        for u in range(2):
+            nc.vector.tensor_copy(d_codes[:, S * u : S * (u + 1)], d_table[:].indirect(k1_l[:, 16 * u : 16 * (u + 1)]))
+        put_back(1)
+        fetch_pairs(3)
+        put_back(2)
+        put_back(3)
 
         z_codes = keep.tile([P, S], U32, name="z_codes", align_bytes=64)
         z_plane = keep.tile([P, S], U8, name="z_plane", align_bytes=64)

@@ -61,12 +61,12 @@ def tile_picked_dhqfillsendtwo_none_p_kernel(
         hz_l = load_list(hz, "hz_l")
         load_scale_rows(nc.sync, x_scale_table, x_scales)
 
-        x_table = keep.tile([P, T], U32, name="x_table")
-        nc.scalar.dma_start(x_table[:].bitcast(I32), x_words[0].rearrange("p n t -> p (n t)").bitcast(I32))
-        k1_l = load_list(k1, "k1_l")
-        n1_l = load_list(n1, "n1_l")
         w1_raw = keep.tile([P, PACK, H], F32, name="w1_raw", tag="wide")
         nc.sync.dma_start(w1_raw[:], w1.rearrange("(p j) c -> p j c", j=PACK))
+        k1_l = load_list(k1, "k1_l")
+        n1_l = load_list(n1, "n1_l")
+        x_table = keep.tile([P, T], U32, name="x_table")
+        nc.sync.dma_start(x_table[:].bitcast(I32), x_words[0].rearrange("p n t -> p (n t)").bitcast(I32))
         w2_rows = w2.rearrange("(p j) c -> p j c", j=PACK)
         w2_head = keep.tile([P, PACK, 384], F32, name="w2_head")
         nc.sync.dma_start(w2_head[:], w2_rows[:, :, 0:384])
@@ -89,19 +89,19 @@ def tile_picked_dhqfillsendtwo_none_p_kernel(
         x_plane = keep.tile([P, 2 * S], U8, name="x_plane", align_bytes=64)
         place_scale_rows(nc.scalar, x_plane, x_scale_picked)
 
+
+        w1_bf = keep.tile([P, PACK * H], BF16, name="w1_bf", align_bytes=64)
+        w2_bf = keep.tile([P, PACK * H], BF16, name="w2_bf", align_bytes=64)
+        round_weight(scalar_round, w1_bf, w1_raw, 0, 0, 32)
+        round_weight(nc.vector.tensor_copy, w1_bf, w1_raw, 0, 32, 128)
+
+        d_table = keep.tile([P, G], U32, name="d_table", tag="wide")
+        nc.sync.dma_start(d_table[:].bitcast(I32), d_words[0].rearrange("p n t -> p (n t)").bitcast(I32))
+
         x_a = keep.tile([P, S], U32, name="x_a", align_bytes=64)
         x_b = keep.tile([P, S], U32, name="x_b", align_bytes=64)
         nc.vector.tensor_copy(x_a[:], x_table[:].indirect(offs_l[:]))
         nc.vector.tensor_copy(x_b[:], x_table[:].indirect(hz_l[:]))
-
-
-        w1_bf = keep.tile([P, PACK * H], BF16, name="w1_bf", align_bytes=64)
-        w2_bf = keep.tile([P, PACK * H], BF16, name="w2_bf", align_bytes=64)
-        round_weight(scalar_round, w1_bf, w1_raw, 0, 0, 56)
-        round_weight(nc.vector.tensor_copy, w1_bf, w1_raw, 0, 56, 128)
-
-        d_table = keep.tile([P, G], U32, name="d_table", tag="wide")
-        nc.sync.dma_start(d_table[:].bitcast(I32), d_words[0].rearrange("p n t -> p (n t)").bitcast(I32))
 
         w1_codes = keep.tile([P, H], U32, name="w1_codes", align_bytes=64)
         w1_plane = keep.tile([P, H], U8, name="w1_plane", align_bytes=64)
@@ -113,63 +113,71 @@ def tile_picked_dhqfillsendtwo_none_p_kernel(
 
         w2_codes = keep.tile([P, H], U32, name="w2_codes", align_bytes=64)
         w2_plane = keep.tile([P, H], U8, name="w2_plane", align_bytes=64)
-        y_banks = [psum.tile([P, S], F32, name=f"y_bank{t}", tag=f"bank{t}") for t in range(PACK)]
+        ys = [keep.tile([P, S], F32, name=f"y{t}") for t in range(PACK)]
         for t in range(PACK):
             cols = slice(P * t, P * (t + 1))
+            bank = psum.tile([P, S], F32, name=f"y_bank{t}", tag=f"bank{t % 2}")
             nc.tensor.matmul_mx(
-                y_banks[t][:], lhsT=w1_codes[:, cols].bitcast(FP8X4), lhsT_scale=w1_plane[:, cols],
+                bank[:], lhsT=w1_codes[:, cols].bitcast(FP8X4), lhsT_scale=w1_plane[:, cols],
                 rhs=x_a[:].bitcast(FP8X4), rhs_scale=x_plane[:, 0:S], start=True, stop=False,
             )
-        for t in range(PACK):
-            cols = slice(P * t, P * (t + 1))
             nc.vector.quantize_mx(
                 w2_codes[:, cols].bitcast(FP8X4), w2_plane[:, cols], w2_bf[:, H * t : H * (t + 1)]
             )
             nc.tensor.matmul_mx(
-                y_banks[t][:], lhsT=w2_codes[:, cols].bitcast(FP8X4), lhsT_scale=w2_plane[:, cols],
+                bank[:], lhsT=w2_codes[:, cols].bitcast(FP8X4), lhsT_scale=w2_plane[:, cols],
                 rhs=x_b[:].bitcast(FP8X4), rhs_scale=x_plane[:, S : 2 * S], start=False, stop=True,
             )
+            if t == 0:
+                nc.scalar.copy(ys[t][:], bank[:])
+            else:
+                nc.vector.tensor_copy(ys[t][:], bank[:])
 
         z_bf = [keep.tile([P, W, PACK], BF16, name=f"z_bf{u}", align_bytes=64) for u in range(2)]
-        ys, larger = [], []
+        larger, d_codes, d_planes = [], [], []
 
         def fetch_pairs(t):
-            y = keep.tile([P, S], F32, name=f"y{t}")
-            if t == 0:
-                nc.scalar.copy(y[:], y_banks[t][:])
-            else:
-                nc.vector.tensor_copy(y[:], y_banks[t][:])
             pa = keep.tile([P, W], F32, name=f"pa{t}", tag=f"pa{t}", align_bytes=64)
             pb = keep.tile([P, W], F32, name=f"pb{t}")
-            nc.scalar.activation(pa[:], y[:].indirect(n1_l[:]), COPY)
-            nc.scalar.activation(pb[:], y[:].indirect(n2_l[:]), COPY)
-            ra = keep.tile([P, W], F32, name=f"ra{t}", tag="wide" if t == 3 else f"ra{t}")
+            nc.scalar.activation(pa[:], ys[t][:].indirect(n1_l[:]), COPY)
+            nc.scalar.activation(pb[:], ys[t][:].indirect(n2_l[:]), COPY)
+            ra = keep.tile([P, W], F32, name=f"ra{t}")
             nc.vector.tensor_tensor(ra[:], pa[:], pb[:], MAX)
-            ys.append(y)
             larger.append(ra)
 
         def put_back(t):
             nc.scalar.activation(ys[t][:].indirect(n1_l[:]), larger[t][:], COPY)
+
+        def weigh(t):
             for u in range(2):
                 nc.vector.tensor_scalar(
                     z_bf[u][:, :, t], ys[t][:, W * u : W * (u + 1)], gain[:, t : t + 1], None, MULT
                 )
 
+        def pick_d_scales(u, tag):
+            picked = keep.tile([P, S], U8, name=f"d_scale_picked{u}", tag=tag, align_bytes=64)
+            nc.vector.tensor_copy(picked[:], d_scale_table[:].indirect(k1_l[:, 16 * u : 16 * (u + 1)]))
+            plane = keep.tile([P, S], U8, name=f"d_plane{u}", align_bytes=64)
+            place_scale_rows(nc.sync, plane, picked)
+            d_planes.append(plane)
+
+        def pick_d_words(u, tag):
+            codes = keep.tile([P, S], U32, name=f"d_codes{u}", tag=tag, align_bytes=64)
+            nc.vector.tensor_copy(codes[:], d_table[:].indirect(k1_l[:, 16 * u : 16 * (u + 1)]))
+            d_codes.append(codes)
+
         fetch_pairs(0)
         fetch_pairs(1)
-        d_scale_picked = keep.tile([P, H], U8, name="d_scale_picked", tag="pa0", align_bytes=64)
-        nc.vector.tensor_copy(d_scale_picked[:], d_scale_table[:].indirect(k1_l[:]))
-        d_plane = keep.tile([P, H], U8, name="d_plane", align_bytes=64)
-        place_scale_rows(nc.sync, d_plane, d_scale_picked)
+        pick_d_scales(0, "pa0")
         put_back(0)
         fetch_pairs(2)
-        d_codes = keep.tile([P, H], U32, name="d_codes", align_bytes=64)
-        for u in range(2):
-            nc.vector.tensor_copy(d_codes[:, S * u : S * (u + 1)], d_table[:].indirect(k1_l[:, 16 * u : 16 * (u + 1)]))
+        pick_d_words(0, "pa1")
         put_back(1)
         fetch_pairs(3)
         put_back(2)
         put_back(3)
+        for t in range(PACK):
+            weigh(t)
 
         z_codes = keep.tile([P, S], U32, name="z_codes", align_bytes=64)
         z_plane = keep.tile([P, S], U8, name="z_plane", align_bytes=64)
@@ -180,9 +188,9 @@ def tile_picked_dhqfillsendtwo_none_p_kernel(
             )
 
         def product(bank, m, cols):
-            rows = slice(P * m, P * (m + 1))
+            rows = slice(P * (m % 2), P * (m % 2 + 1))
             nc.tensor.matmul_mx(
-                bank[:], lhsT=d_codes[:, rows].bitcast(FP8X4), lhsT_scale=d_plane[:, rows],
+                bank[:], lhsT=d_codes[m // 2][:, rows].bitcast(FP8X4), lhsT_scale=d_planes[m // 2][:, rows],
                 rhs=z_codes[:, cols].bitcast(FP8X4), rhs_scale=z_plane[:, cols], start=True, stop=True,
             )
 
@@ -194,9 +202,9 @@ def tile_picked_dhqfillsendtwo_none_p_kernel(
         sent3 = keep.tile([P, S], F32, name="sent3_0")
         sent4 = keep.tile([P, S], F32, name="sent4_0")
         for u in range(2):
-            bank = psum.tile([P, W], F32, name=f"h_bank0_{u}", tag=f"bank{4 + u}")
+            bank = psum.tile([P, W], F32, name=f"h_bank0_{u}", tag=f"bank{2 + u}")
             product(bank, 0, slice(W * u, W * (u + 1)))
-            h = keep.tile([P, W], F32, name=f"h0_{u}")
+            h = keep.tile([P, W], F32, name=f"h0_{u}", tag=f"h0_{u}", align_bytes=64)
             if u == 0:
                 nc.scalar.activation(h[:], bank[:], COPY, scale=0.0625)
             else:
@@ -206,7 +214,10 @@ def tile_picked_dhqfillsendtwo_none_p_kernel(
         finish(0, sent3, sent4)
 
         for m in range(1, PACK):
-            bank = psum.tile([P, S], F32, name=f"h_bank{m}", tag=f"bank{(5 + m) % 8}")
+            if m == 2:
+                pick_d_scales(1, "h0_0")
+                pick_d_words(1, "h0_1")
+            bank = psum.tile([P, S], F32, name=f"h_bank{m}", tag=f"bank{3 + m}")
             product(bank, m, slice(0, S))
             h = keep.tile([P, S], F32, name=f"h{m}")
             nc.vector.tensor_scalar(h[:], bank[:], 0.0625, None, MULT)

@@ -57,16 +57,20 @@ def tile_picked_dhqfillsendtwo_none_p_kernel(
 
         x_scale_table = keep.tile([P, T], U8, name="x_scale_table")
 
+        warm = keep.tile([P, 16], F32, name="warm")
+        nc.vector.memset(warm[:, 0:8], 0.0)
+        nc.scalar.activation(warm[:, 8:16], warm[:, 0:8], COPY)
+
         offs_l = load_list(offs, "offs_l")
         hz_l = load_list(hz, "hz_l")
         load_scale_rows(nc.sync, x_scale_table, x_scales)
 
-        w1_raw = keep.tile([P, PACK, H], F32, name="w1_raw", tag="wide")
-        nc.sync.dma_start(w1_raw[:], w1.rearrange("(p j) c -> p j c", j=PACK))
+        x_table = keep.tile([P, T], U32, name="x_table")
+        nc.scalar.dma_start(x_table[:].bitcast(I32), x_words[0].rearrange("p n t -> p (n t)").bitcast(I32))
         k1_l = load_list(k1, "k1_l")
         n1_l = load_list(n1, "n1_l")
-        x_table = keep.tile([P, T], U32, name="x_table")
-        nc.sync.dma_start(x_table[:].bitcast(I32), x_words[0].rearrange("p n t -> p (n t)").bitcast(I32))
+        w1_raw = keep.tile([P, PACK, H], F32, name="w1_raw", tag="wide")
+        nc.sync.dma_start(w1_raw[:], w1.rearrange("(p j) c -> p j c", j=PACK))
         w2_rows = w2.rearrange("(p j) c -> p j c", j=PACK)
         w2_head = keep.tile([P, PACK, 384], F32, name="w2_head")
         nc.sync.dma_start(w2_head[:], w2_rows[:, :, 0:384])
@@ -89,19 +93,19 @@ def tile_picked_dhqfillsendtwo_none_p_kernel(
         x_plane = keep.tile([P, 2 * S], U8, name="x_plane", align_bytes=64)
         place_scale_rows(nc.scalar, x_plane, x_scale_picked)
 
-
-        w1_bf = keep.tile([P, PACK * H], BF16, name="w1_bf", align_bytes=64)
-        w2_bf = keep.tile([P, PACK * H], BF16, name="w2_bf", align_bytes=64)
-        round_weight(scalar_round, w1_bf, w1_raw, 0, 0, 32)
-        round_weight(nc.vector.tensor_copy, w1_bf, w1_raw, 0, 32, 128)
-
-        d_table = keep.tile([P, G], U32, name="d_table", tag="wide")
-        nc.sync.dma_start(d_table[:].bitcast(I32), d_words[0].rearrange("p n t -> p (n t)").bitcast(I32))
-
         x_a = keep.tile([P, S], U32, name="x_a", align_bytes=64)
         x_b = keep.tile([P, S], U32, name="x_b", align_bytes=64)
         nc.vector.tensor_copy(x_a[:], x_table[:].indirect(offs_l[:]))
         nc.vector.tensor_copy(x_b[:], x_table[:].indirect(hz_l[:]))
+
+
+        w1_bf = keep.tile([P, PACK * H], BF16, name="w1_bf", align_bytes=64)
+        w2_bf = keep.tile([P, PACK * H], BF16, name="w2_bf", align_bytes=64)
+        round_weight(scalar_round, w1_bf, w1_raw, 0, 0, 56)
+        round_weight(nc.vector.tensor_copy, w1_bf, w1_raw, 0, 56, 128)
+
+        d_table = keep.tile([P, G], U32, name="d_table", tag="wide")
+        nc.sync.dma_start(d_table[:].bitcast(I32), d_words[0].rearrange("p n t -> p (n t)").bitcast(I32))
 
         w1_codes = keep.tile([P, H], U32, name="w1_codes", align_bytes=64)
         w1_plane = keep.tile([P, H], U8, name="w1_plane", align_bytes=64)
@@ -134,7 +138,7 @@ def tile_picked_dhqfillsendtwo_none_p_kernel(
                 nc.vector.tensor_copy(ys[t][:], bank[:])
 
         z_bf = [keep.tile([P, W, PACK], BF16, name=f"z_bf{u}", align_bytes=64) for u in range(2)]
-        larger, d_codes, d_planes = [], [], []
+        larger, d_codes = [], []
 
         def fetch_pairs(t):
             pa = keep.tile([P, W], F32, name=f"pa{t}", tag=f"pa{t}", align_bytes=64)
@@ -154,13 +158,6 @@ def tile_picked_dhqfillsendtwo_none_p_kernel(
                     z_bf[u][:, :, t], ys[t][:, W * u : W * (u + 1)], gain[:, t : t + 1], None, MULT
                 )
 
-        def pick_d_scales(u, tag):
-            picked = keep.tile([P, S], U8, name=f"d_scale_picked{u}", tag=tag, align_bytes=64)
-            nc.vector.tensor_copy(picked[:], d_scale_table[:].indirect(k1_l[:, 16 * u : 16 * (u + 1)]))
-            plane = keep.tile([P, S], U8, name=f"d_plane{u}", align_bytes=64)
-            place_scale_rows(nc.sync, plane, picked)
-            d_planes.append(plane)
-
         def pick_d_words(u, tag):
             codes = keep.tile([P, S], U32, name=f"d_codes{u}", tag=tag, align_bytes=64)
             nc.vector.tensor_copy(codes[:], d_table[:].indirect(k1_l[:, 16 * u : 16 * (u + 1)]))
@@ -168,7 +165,10 @@ def tile_picked_dhqfillsendtwo_none_p_kernel(
 
         fetch_pairs(0)
         fetch_pairs(1)
-        pick_d_scales(0, "pa0")
+        d_scale_picked = keep.tile([P, H], U8, name="d_scale_picked", tag="pa0", align_bytes=64)
+        nc.vector.tensor_copy(d_scale_picked[:], d_scale_table[:].indirect(k1_l[:]))
+        d_plane = keep.tile([P, H], U8, name="d_plane", align_bytes=64)
+        place_scale_rows(nc.sync, d_plane, d_scale_picked)
         put_back(0)
         fetch_pairs(2)
         pick_d_words(0, "pa1")
@@ -190,7 +190,7 @@ def tile_picked_dhqfillsendtwo_none_p_kernel(
         def product(bank, m, cols):
             rows = slice(P * (m % 2), P * (m % 2 + 1))
             nc.tensor.matmul_mx(
-                bank[:], lhsT=d_codes[m // 2][:, rows].bitcast(FP8X4), lhsT_scale=d_planes[m // 2][:, rows],
+                bank[:], lhsT=d_codes[m // 2][:, rows].bitcast(FP8X4), lhsT_scale=d_plane[:, P * m : P * (m + 1)],
                 rhs=z_codes[:, cols].bitcast(FP8X4), rhs_scale=z_plane[:, cols], start=True, stop=True,
             )
 
@@ -215,7 +215,6 @@ def tile_picked_dhqfillsendtwo_none_p_kernel(
 
         for m in range(1, PACK):
             if m == 2:
-                pick_d_scales(1, "h0_0")
                 pick_d_words(1, "h0_1")
             bank = psum.tile([P, S], F32, name=f"h_bank{m}", tag=f"bank{3 + m}")
             product(bank, m, slice(0, S))

@@ -18,6 +18,13 @@ MAX = mybir.AluOpType.max
 
 P = 128
 PACK = 4
+GROUP = 16
+QUADRANT = 32
+BLOCKS = 16
+MX_ALIGN = 64
+H_SCALE = 0.0625
+W2_TAIL = 128
+W2_HEAD = H - W2_TAIL
 
 
 def tile_picked_dhqfillsendtwo_none_p_kernel(
@@ -34,114 +41,113 @@ def tile_picked_dhqfillsendtwo_none_p_kernel(
             nc.sync.dma_start(tile[:], src)
             return tile
 
-        def load_scale_rows(queue, table, scales):
-            rows = scales[0].bitcast(I32)
-            words = rows.shape[1]
-            for r in range(2):
-                queue.dma_start(
-                    table[r:P:2, :].bitcast(I32), rows[r:16:2, :].unsqueeze(1).to_broadcast([8, 8, words])
-                )
-
-        def place_scale_rows(queue, plane, picked):
+        def make_plane(queue, plane, picked):
             nc.vector.tensor_copy(plane[:].bitcast(I32), picked[:].bitcast(I32))
             for r in range(2):
-                queue.dma_start(plane[2 + r : P : 32, :].bitcast(I32), picked[16 + r : P : 32, :].bitcast(I32))
+                queue.dma_start(
+                    plane[2 + r : P : QUADRANT, :].bitcast(I32), picked[GROUP + r : P : QUADRANT, :].bitcast(I32)
+                )
 
         def scalar_round(dst, src):
             nc.scalar.activation(dst, src, COPY)
 
-        def round_weight(engine_copy, grouped, raw, raw_m0, m0, m1):
+        def dealt(raw, rounded):
             src = raw[:].rearrange("p j (m t) -> p m j t", t=PACK)
-            dst = grouped[:].rearrange("p (t m j) -> p m j t", t=PACK, j=PACK)
-            engine_copy(dst[:, m0:m1], src[:, m0 - raw_m0 : m1 - raw_m0])
+            return src, rounded[:].rearrange("p (t m j) -> p m j t", m=P, j=PACK)
 
         x_scale_table = keep.tile([P, T], U8, name="x_scale_table")
-
-        warm = keep.tile([P, 16], F32, name="warm")
-        nc.vector.memset(warm[:, 0:8], 0.0)
-        nc.scalar.activation(warm[:, 8:16], warm[:, 0:8], COPY)
-
         offs_l = load_list(offs, "offs_l")
         hz_l = load_list(hz, "hz_l")
-        load_scale_rows(nc.sync, x_scale_table, x_scales)
-
+        x_rows = x_scales[0].bitcast(I32)
+        for r in range(2):
+            nc.sync.dma_start(
+                x_scale_table[r:P:2, :].bitcast(I32),
+                x_rows[r:BLOCKS:2, :].unsqueeze(1).to_broadcast([P // GROUP, GROUP // 2, T // 4]),
+            )
         x_table = keep.tile([P, T], U32, name="x_table")
         nc.scalar.dma_start(x_table[:].bitcast(I32), x_words[0].rearrange("p n t -> p (n t)").bitcast(I32))
         k1_l = load_list(k1, "k1_l")
         n1_l = load_list(n1, "n1_l")
-        w1_raw = keep.tile([P, PACK, H], F32, name="w1_raw", tag="wide")
+        w1_raw = keep.tile([P, PACK, H], F32, name="w1_raw", tag="w1_then_d")
         nc.sync.dma_start(w1_raw[:], w1.rearrange("(p j) c -> p j c", j=PACK))
         w2_rows = w2.rearrange("(p j) c -> p j c", j=PACK)
-        w2_head = keep.tile([P, PACK, 384], F32, name="w2_head")
-        nc.sync.dma_start(w2_head[:], w2_rows[:, :, 0:384])
-        w2_tail = keep.tile([P, PACK, 128], F32, name="w2_tail")
-        nc.sync.dma_start(w2_tail[:], w2_rows[:, :, 384:512])
-
+        w2_head = keep.tile([P, PACK, W2_HEAD], F32, name="w2_head")
+        nc.sync.dma_start(w2_head[:], w2_rows[:, :, 0:W2_HEAD])
+        w2_tail = keep.tile([P, PACK, W2_TAIL], F32, name="w2_tail")
+        nc.sync.dma_start(w2_tail[:], w2_rows[:, :, W2_HEAD:H])
         n2_l = load_list(n2, "n2_l")
         n3_l = load_list(n3, "n3_l")
         n4_l = load_list(n4, "n4_l")
         d_scale_table = keep.tile([P, G], U8, name="d_scale_table")
         nc.gpsimd.memset(d_scale_table[:].bitcast(I32), 0)
         for r in range(2):
-            nc.gpsimd.dma_start(d_scale_table[r:P:16, :].bitcast(I32), d_scales[0].bitcast(I32)[r:16:2, :])
+            nc.gpsimd.dma_start(d_scale_table[r:P:GROUP, :].bitcast(I32), d_scales[0].bitcast(I32)[r:BLOCKS:2, :])
         gain = keep.tile([P, PACK], F32, name="gain")
         nc.gpsimd.dma_start(gain[:], gs.rearrange("(p t) o -> p (t o)", t=PACK))
 
         x_scale_picked = keep.tile([P, 2 * S], U8, name="x_scale_picked")
         nc.vector.tensor_copy(x_scale_picked[:, 0:S], x_scale_table[:].indirect(offs_l[:]))
         nc.vector.tensor_copy(x_scale_picked[:, S : 2 * S], x_scale_table[:].indirect(hz_l[:]))
-        x_plane = keep.tile([P, 2 * S], U8, name="x_plane", align_bytes=64)
-        place_scale_rows(nc.scalar, x_plane, x_scale_picked)
+        x_plane = keep.tile([P, 2 * S], U8, name="x_plane", align_bytes=MX_ALIGN)
+        make_plane(nc.scalar, x_plane, x_scale_picked)
+        x_by_offs = keep.tile([P, S], U32, name="x_by_offs", align_bytes=MX_ALIGN)
+        x_by_hz = keep.tile([P, S], U32, name="x_by_hz", align_bytes=MX_ALIGN)
+        nc.vector.tensor_copy(x_by_offs[:], x_table[:].indirect(offs_l[:]))
+        nc.vector.tensor_copy(x_by_hz[:], x_table[:].indirect(hz_l[:]))
 
-        x_a = keep.tile([P, S], U32, name="x_a", align_bytes=64)
-        x_b = keep.tile([P, S], U32, name="x_b", align_bytes=64)
-        nc.vector.tensor_copy(x_a[:], x_table[:].indirect(offs_l[:]))
-        nc.vector.tensor_copy(x_b[:], x_table[:].indirect(hz_l[:]))
+        last = PACK - 1
+        w1_bf = keep.tile([P, last * H], BF16, name="w1_bf", align_bytes=MX_ALIGN)
+        w1_bf_last = keep.tile([P, H], BF16, name="w1_bf_last", align_bytes=MX_ALIGN)
+        w2_bf = keep.tile([P, PACK * H], BF16, name="w2_bf", align_bytes=MX_ALIGN)
+        src, dst = dealt(w1_raw, w1_bf_last)
+        scalar_round(dst, src[:, :, :, last:PACK])
+        src, dst = dealt(w1_raw, w1_bf)
+        nc.vector.tensor_copy(dst, src[:, :, :, 0:last])
 
-
-        w1_bf = keep.tile([P, PACK * H], BF16, name="w1_bf", align_bytes=64)
-        w2_bf = keep.tile([P, PACK * H], BF16, name="w2_bf", align_bytes=64)
-        round_weight(scalar_round, w1_bf, w1_raw, 0, 0, 56)
-        round_weight(nc.vector.tensor_copy, w1_bf, w1_raw, 0, 56, 128)
-
-        d_table = keep.tile([P, G], U32, name="d_table", tag="wide")
+        d_table = keep.tile([P, G], U32, name="d_table", tag="w1_then_d")
         nc.sync.dma_start(d_table[:].bitcast(I32), d_words[0].rearrange("p n t -> p (n t)").bitcast(I32))
 
-        w1_codes = keep.tile([P, H], U32, name="w1_codes", align_bytes=64)
-        w1_plane = keep.tile([P, H], U8, name="w1_plane", align_bytes=64)
-        nc.vector.quantize_mx(w1_codes[:].bitcast(FP8X4), w1_plane[:], w1_bf[:])
+        w1_codes = keep.tile([P, H], U32, name="w1_codes", align_bytes=MX_ALIGN)
+        w1_plane = keep.tile([P, H], U8, name="w1_plane", align_bytes=MX_ALIGN)
+        nc.vector.quantize_mx(w1_codes[:, 0 : last * P].bitcast(FP8X4), w1_plane[:, 0 : last * P], w1_bf[:])
 
-        round_weight(nc.vector.tensor_copy, w2_bf, w2_head, 0, 0, 48)
-        round_weight(scalar_round, w2_bf, w2_head, 0, 48, 96)
-        round_weight(nc.vector.tensor_copy, w2_bf, w2_tail, 96, 96, 128)
+        head = W2_HEAD // PACK
+        src, dst = dealt(w2_head, w2_bf)
+        nc.vector.tensor_copy(dst[:, 0:head], src)
+        src, dst = dealt(w2_tail, w2_bf)
+        nc.vector.tensor_copy(dst[:, head:P], src)
 
-        w2_codes = keep.tile([P, H], U32, name="w2_codes", align_bytes=64)
-        w2_plane = keep.tile([P, H], U8, name="w2_plane", align_bytes=64)
+        w2_codes = keep.tile([P, H], U32, name="w2_codes", align_bytes=MX_ALIGN)
+        w2_plane = keep.tile([P, H], U8, name="w2_plane", align_bytes=MX_ALIGN)
         ys = [keep.tile([P, S], F32, name=f"y{t}") for t in range(PACK)]
         for t in range(PACK):
             cols = slice(P * t, P * (t + 1))
-            bank = psum.tile([P, S], F32, name=f"y_bank{t}", tag=f"bank{t % 2}")
+            bank = psum.tile([P, S], F32, name=f"y_bank{t}", tag=f"y_bank{t % 2}")
+            if t == last:
+                nc.vector.quantize_mx(w1_codes[:, cols].bitcast(FP8X4), w1_plane[:, cols], w1_bf_last[:])
             nc.tensor.matmul_mx(
                 bank[:], lhsT=w1_codes[:, cols].bitcast(FP8X4), lhsT_scale=w1_plane[:, cols],
-                rhs=x_a[:].bitcast(FP8X4), rhs_scale=x_plane[:, 0:S], start=True, stop=False,
+                rhs=x_by_offs[:].bitcast(FP8X4), rhs_scale=x_plane[:, 0:S], start=True, stop=False,
             )
             nc.vector.quantize_mx(
                 w2_codes[:, cols].bitcast(FP8X4), w2_plane[:, cols], w2_bf[:, H * t : H * (t + 1)]
             )
             nc.tensor.matmul_mx(
                 bank[:], lhsT=w2_codes[:, cols].bitcast(FP8X4), lhsT_scale=w2_plane[:, cols],
-                rhs=x_b[:].bitcast(FP8X4), rhs_scale=x_plane[:, S : 2 * S], start=False, stop=True,
+                rhs=x_by_hz[:].bitcast(FP8X4), rhs_scale=x_plane[:, S : 2 * S], start=False, stop=True,
             )
             if t == 0:
                 nc.scalar.copy(ys[t][:], bank[:])
             else:
                 nc.vector.tensor_copy(ys[t][:], bank[:])
 
-        z_bf = [keep.tile([P, W, PACK], BF16, name=f"z_bf{u}", align_bytes=64) for u in range(2)]
+        z_bf = [
+            keep.tile([P, W, PACK], BF16, name=f"z_bf{u}", tag=f"z_bf{u}", align_bytes=MX_ALIGN) for u in range(2)
+        ]
         larger, d_codes = [], []
 
         def fetch_pairs(t):
-            pa = keep.tile([P, W], F32, name=f"pa{t}", tag=f"pa{t}", align_bytes=64)
+            pa = keep.tile([P, W], F32, name=f"pa{t}", tag=f"pa{t}", align_bytes=MX_ALIGN)
             pb = keep.tile([P, W], F32, name=f"pb{t}")
             nc.scalar.activation(pa[:], ys[t][:].indirect(n1_l[:]), COPY)
             nc.scalar.activation(pb[:], ys[t][:].indirect(n2_l[:]), COPY)
@@ -159,16 +165,17 @@ def tile_picked_dhqfillsendtwo_none_p_kernel(
                 )
 
         def pick_d_words(u, tag):
-            codes = keep.tile([P, S], U32, name=f"d_codes{u}", tag=tag, align_bytes=64)
-            nc.vector.tensor_copy(codes[:], d_table[:].indirect(k1_l[:, 16 * u : 16 * (u + 1)]))
+            codes = keep.tile([P, S], U32, name=f"d_codes{u}", tag=tag, align_bytes=MX_ALIGN)
+            entries = slice(S // GROUP * u, S // GROUP * (u + 1))
+            nc.vector.tensor_copy(codes[:], d_table[:].indirect(k1_l[:, entries]))
             d_codes.append(codes)
 
         fetch_pairs(0)
         fetch_pairs(1)
-        d_scale_picked = keep.tile([P, H], U8, name="d_scale_picked", tag="pa0", align_bytes=64)
+        d_scale_picked = keep.tile([P, H], U8, name="d_scale_picked", tag="pa0", align_bytes=MX_ALIGN)
         nc.vector.tensor_copy(d_scale_picked[:], d_scale_table[:].indirect(k1_l[:]))
-        d_plane = keep.tile([P, H], U8, name="d_plane", align_bytes=64)
-        place_scale_rows(nc.sync, d_plane, d_scale_picked)
+        d_plane = keep.tile([P, H], U8, name="d_plane", align_bytes=MX_ALIGN)
+        make_plane(nc.sync, d_plane, d_scale_picked)
         put_back(0)
         fetch_pairs(2)
         pick_d_words(0, "pa1")
@@ -179,8 +186,8 @@ def tile_picked_dhqfillsendtwo_none_p_kernel(
         for t in range(PACK):
             weigh(t)
 
-        z_codes = keep.tile([P, S], U32, name="z_codes", align_bytes=64)
-        z_plane = keep.tile([P, S], U8, name="z_plane", align_bytes=64)
+        z_codes = keep.tile([P, S], U32, name="z_codes", align_bytes=MX_ALIGN)
+        z_plane = keep.tile([P, S], U8, name="z_plane", align_bytes=MX_ALIGN)
         for u in range(2):
             cols = slice(W * u, W * (u + 1))
             nc.vector.quantize_mx(
@@ -194,34 +201,34 @@ def tile_picked_dhqfillsendtwo_none_p_kernel(
                 rhs=z_codes[:, cols].bitcast(FP8X4), rhs_scale=z_plane[:, cols], start=True, stop=True,
             )
 
-        def finish(m, sent3, sent4):
+        def finish(m, ds2, ds3):
             res = keep.tile([P, S], F32, name=f"res{m}")
-            nc.vector.tensor_tensor(res[:], sent3[:, 0:S], sent4[:, 0:S], MAX)
+            nc.vector.tensor_tensor(res[:], ds2[:, 0:S], ds3[:, 0:S], MAX)
             nc.sync.dma_start(out[P * m : P * (m + 1), :], res[:])
 
-        sent3 = keep.tile([P, S], F32, name="sent3_0")
-        sent4 = keep.tile([P, S], F32, name="sent4_0")
+        ds2 = keep.tile([P, S], F32, name="ds2_0")
+        ds3 = keep.tile([P, S], F32, name="ds3_0")
         for u in range(2):
-            bank = psum.tile([P, W], F32, name=f"h_bank0_{u}", tag=f"bank{2 + u}")
+            bank = psum.tile([P, W], F32, name=f"h_bank0_{u}")
             product(bank, 0, slice(W * u, W * (u + 1)))
-            h = keep.tile([P, W], F32, name=f"h0_{u}", tag=f"h0_{u}", align_bytes=64)
+            h = keep.tile([P, W], F32, name=f"h0_{u}")
             if u == 0:
-                nc.scalar.activation(h[:], bank[:], COPY, scale=0.0625)
+                nc.scalar.activation(h[:], bank[:], COPY, scale=H_SCALE)
             else:
-                nc.vector.tensor_scalar(h[:], bank[:], 0.0625, None, MULT)
-            nc.scalar.activation(sent3[:].indirect(n3_l[:, 8 * u : 8 * (u + 1)]), h[:], COPY)
-            nc.scalar.activation(sent4[:].indirect(n4_l[:, 8 * u : 8 * (u + 1)]), h[:], COPY)
-        finish(0, sent3, sent4)
+                nc.vector.tensor_scalar(h[:], bank[:], H_SCALE, None, MULT)
+            entries = slice(W // GROUP * u, W // GROUP * (u + 1))
+            nc.scalar.activation(ds2[:].indirect(n3_l[:, entries]), h[:], COPY)
+            nc.scalar.activation(ds3[:].indirect(n4_l[:, entries]), h[:], COPY)
+        pick_d_words(1, "z_bf1")
+        finish(0, ds2, ds3)
 
         for m in range(1, PACK):
-            if m == 2:
-                pick_d_words(1, "h0_1")
-            bank = psum.tile([P, S], F32, name=f"h_bank{m}", tag=f"bank{3 + m}")
+            bank = psum.tile([P, S], F32, name=f"h_bank{m}")
             product(bank, m, slice(0, S))
             h = keep.tile([P, S], F32, name=f"h{m}")
-            nc.vector.tensor_scalar(h[:], bank[:], 0.0625, None, MULT)
-            sent3 = keep.tile([P, 2 * S], F32, name=f"sent3_{m}")
-            sent4 = keep.tile([P, 2 * S], F32, name=f"sent4_{m}")
-            nc.scalar.activation(sent3[:].indirect(n3_l[:]), h[:], COPY)
-            nc.scalar.activation(sent4[:].indirect(n4_l[:]), h[:], COPY)
-            finish(m, sent3, sent4)
+            nc.vector.tensor_scalar(h[:], bank[:], H_SCALE, None, MULT)
+            ds2 = keep.tile([P, 2 * S], F32, name=f"ds2_{m}")
+            ds3 = keep.tile([P, 2 * S], F32, name=f"ds3_{m}")
+            nc.scalar.activation(ds2[:].indirect(n3_l[:]), h[:], COPY)
+            nc.scalar.activation(ds3[:].indirect(n4_l[:]), h[:], COPY)
+            finish(m, ds2, ds3)

from contextlib import ExitStack

import concourse.mybir as mybir

K, T, S, H, W, G = 512, 1024, 256, 512, 128, 2048
FLOPS = 2 * K * H * S * 3

F32 = mybir.dt.float32
BF16 = mybir.dt.bfloat16
I32 = mybir.dt.int32
U32 = mybir.dt.uint32
U16 = mybir.dt.uint16
U8 = mybir.dt.uint8
FP8X4 = mybir.dt.float8_e4m3fn_x4
COPY = mybir.ActivationFunctionType.Copy
MULT = mybir.AluOpType.mult
MAX = mybir.AluOpType.max

P = 128
PACK = 4
GROUP = 16
QUADRANT = 32
BLOCKS = 16
MX_ALIGN = 64
H_SCALE = 0.0625
W2_TAIL = 128
W2_HEAD = H - W2_TAIL


def tile_picked_dhqfillsendtwo_none_p_kernel(
    tc, x_words, x_scales, w1, w2, gs, d_words, d_scales, offs, hz, n1, n2, k1, n3, n4, out
):
    nc = tc.nc
    with ExitStack() as ctx:
        lists = ctx.enter_context(tc.tile_pool(name="lists", bufs=1))
        keep = ctx.enter_context(tc.tile_pool(name="keep", bufs=1))
        psum = ctx.enter_context(tc.psum_pool(name="psum", bufs=1))

        def load_list(src, name):
            tile = lists.tile(list(src.shape), U16, name=name)
            nc.sync.dma_start(tile[:], src)
            return tile

        def make_plane(queue, plane, picked):
            nc.vector.tensor_copy(plane[:].bitcast(I32), picked[:].bitcast(I32))
            for r in range(2):
                queue.dma_start(
                    plane[2 + r : P : QUADRANT, :].bitcast(I32), picked[GROUP + r : P : QUADRANT, :].bitcast(I32)
                )

        def scalar_round(dst, src):
            nc.scalar.activation(dst, src, COPY)

        def dealt(raw, rounded):
            src = raw[:].rearrange("p j (m t) -> p m j t", t=PACK)
            return src, rounded[:].rearrange("p (t m j) -> p m j t", m=P, j=PACK)

        x_scale_table = keep.tile([P, T], U8, name="x_scale_table")
        offs_l = load_list(offs, "offs_l")
        hz_l = load_list(hz, "hz_l")
        x_rows = x_scales[0].bitcast(I32)
        for r in range(2):
            nc.sync.dma_start(
                x_scale_table[r:P:2, :].bitcast(I32),
                x_rows[r:BLOCKS:2, :].unsqueeze(1).to_broadcast([P // GROUP, GROUP // 2, T // 4]),
            )
        x_table = keep.tile([P, T], U32, name="x_table")
        nc.scalar.dma_start(x_table[:].bitcast(I32), x_words[0].rearrange("p n t -> p (n t)").bitcast(I32))
        k1_l = load_list(k1, "k1_l")
        n1_l = load_list(n1, "n1_l")
        w1_raw = keep.tile([P, PACK, H], F32, name="w1_raw", tag="w1_then_d")
        nc.sync.dma_start(w1_raw[:], w1.rearrange("(p j) c -> p j c", j=PACK))
        w2_rows = w2.rearrange("(p j) c -> p j c", j=PACK)
        w2_head = keep.tile([P, PACK, W2_HEAD], F32, name="w2_head")
        nc.sync.dma_start(w2_head[:], w2_rows[:, :, 0:W2_HEAD])
        w2_tail = keep.tile([P, PACK, W2_TAIL], F32, name="w2_tail")
        nc.sync.dma_start(w2_tail[:], w2_rows[:, :, W2_HEAD:H])
        n2_l = load_list(n2, "n2_l")
        n3_l = load_list(n3, "n3_l")
        n4_l = load_list(n4, "n4_l")
        d_scale_table = keep.tile([P, G], U8, name="d_scale_table")
        nc.gpsimd.memset(d_scale_table[:].bitcast(I32), 0)
        for r in range(2):
            nc.gpsimd.dma_start(d_scale_table[r:P:GROUP, :].bitcast(I32), d_scales[0].bitcast(I32)[r:BLOCKS:2, :])
        gain = keep.tile([P, PACK], F32, name="gain")
        nc.gpsimd.dma_start(gain[:], gs.rearrange("(p t) o -> p (t o)", t=PACK))

        x_scale_picked = keep.tile([P, 2 * S], U8, name="x_scale_picked")
        nc.vector.tensor_copy(x_scale_picked[:, 0:S], x_scale_table[:].indirect(offs_l[:]))
        nc.vector.tensor_copy(x_scale_picked[:, S : 2 * S], x_scale_table[:].indirect(hz_l[:]))
        x_plane = keep.tile([P, 2 * S], U8, name="x_plane", align_bytes=MX_ALIGN)
        make_plane(nc.scalar, x_plane, x_scale_picked)
        x_by_offs = keep.tile([P, S], U32, name="x_by_offs", align_bytes=MX_ALIGN)
        x_by_hz = keep.tile([P, S], U32, name="x_by_hz", align_bytes=MX_ALIGN)
        nc.vector.tensor_copy(x_by_offs[:], x_table[:].indirect(offs_l[:]))
        nc.vector.tensor_copy(x_by_hz[:], x_table[:].indirect(hz_l[:]))

        last = PACK - 1
        w1_bf = keep.tile([P, last * H], BF16, name="w1_bf", align_bytes=MX_ALIGN)
        w1_bf_last = keep.tile([P, H], BF16, name="w1_bf_last", align_bytes=MX_ALIGN)
        w2_bf = keep.tile([P, PACK * H], BF16, name="w2_bf", align_bytes=MX_ALIGN)
        src, dst = dealt(w1_raw, w1_bf_last)
        scalar_round(dst, src[:, :, :, last:PACK])
        src, dst = dealt(w1_raw, w1_bf)
        nc.vector.tensor_copy(dst, src[:, :, :, 0:last])

        d_table = keep.tile([P, G], U32, name="d_table", tag="w1_then_d")
        nc.sync.dma_start(d_table[:].bitcast(I32), d_words[0].rearrange("p n t -> p (n t)").bitcast(I32))

        w1_codes = keep.tile([P, H], U32, name="w1_codes", align_bytes=MX_ALIGN)
        w1_plane = keep.tile([P, H], U8, name="w1_plane", align_bytes=MX_ALIGN)
        nc.vector.quantize_mx(w1_codes[:, 0 : last * P].bitcast(FP8X4), w1_plane[:, 0 : last * P], w1_bf[:])

        head = W2_HEAD // PACK
        src, dst = dealt(w2_head, w2_bf)
        nc.vector.tensor_copy(dst[:, 0:head], src)
        src, dst = dealt(w2_tail, w2_bf)
        nc.vector.tensor_copy(dst[:, head:P], src)

        w2_codes = keep.tile([P, H], U32, name="w2_codes", align_bytes=MX_ALIGN)
        w2_plane = keep.tile([P, H], U8, name="w2_plane", align_bytes=MX_ALIGN)
        ys = [keep.tile([P, S], F32, name=f"y{t}") for t in range(PACK)]
        for t in range(PACK):
            cols = slice(P * t, P * (t + 1))
            bank = psum.tile([P, S], F32, name=f"y_bank{t}", tag=f"y_bank{t % 2}")
            if t == last:
                nc.vector.quantize_mx(w1_codes[:, cols].bitcast(FP8X4), w1_plane[:, cols], w1_bf_last[:])
            nc.tensor.matmul_mx(
                bank[:], lhsT=w1_codes[:, cols].bitcast(FP8X4), lhsT_scale=w1_plane[:, cols],
                rhs=x_by_offs[:].bitcast(FP8X4), rhs_scale=x_plane[:, 0:S], start=True, stop=False,
            )
            nc.vector.quantize_mx(
                w2_codes[:, cols].bitcast(FP8X4), w2_plane[:, cols], w2_bf[:, H * t : H * (t + 1)]
            )
            nc.tensor.matmul_mx(
                bank[:], lhsT=w2_codes[:, cols].bitcast(FP8X4), lhsT_scale=w2_plane[:, cols],
                rhs=x_by_hz[:].bitcast(FP8X4), rhs_scale=x_plane[:, S : 2 * S], start=False, stop=True,
            )
            if t == 0:
                nc.scalar.copy(ys[t][:], bank[:])
            else:
                nc.vector.tensor_copy(ys[t][:], bank[:])

        z_bf = [
            keep.tile([P, W, PACK], BF16, name=f"z_bf{u}", tag=f"z_bf{u}", align_bytes=MX_ALIGN) for u in range(2)
        ]
        larger, d_codes = [], []

        def fetch_pairs(t):
            pa = keep.tile([P, W], F32, name=f"pa{t}", tag=f"pa{t}", align_bytes=MX_ALIGN)
            pb = keep.tile([P, W], F32, name=f"pb{t}")
            nc.scalar.activation(pa[:], ys[t][:].indirect(n1_l[:]), COPY)
            nc.scalar.activation(pb[:], ys[t][:].indirect(n2_l[:]), COPY)
            ra = keep.tile([P, W], F32, name=f"ra{t}")
            nc.vector.tensor_tensor(ra[:], pa[:], pb[:], MAX)
            larger.append(ra)

        def put_back(t):
            nc.scalar.activation(ys[t][:].indirect(n1_l[:]), larger[t][:], COPY)

        def weigh(t):
            for u in range(2):
                nc.vector.tensor_scalar(
                    z_bf[u][:, :, t], ys[t][:, W * u : W * (u + 1)], gain[:, t : t + 1], None, MULT
                )

        def pick_d_words(u, tag):
            codes = keep.tile([P, S], U32, name=f"d_codes{u}", tag=tag, align_bytes=MX_ALIGN)
            entries = slice(S // GROUP * u, S // GROUP * (u + 1))
            nc.vector.tensor_copy(codes[:], d_table[:].indirect(k1_l[:, entries]))
            d_codes.append(codes)

        fetch_pairs(0)
        fetch_pairs(1)
        d_scale_picked = keep.tile([P, H], U8, name="d_scale_picked", tag="pa0", align_bytes=MX_ALIGN)
        nc.vector.tensor_copy(d_scale_picked[:], d_scale_table[:].indirect(k1_l[:]))
        d_plane = keep.tile([P, H], U8, name="d_plane", align_bytes=MX_ALIGN)
        make_plane(nc.sync, d_plane, d_scale_picked)
        put_back(0)
        fetch_pairs(2)
        pick_d_words(0, "pa1")
        put_back(1)
        fetch_pairs(3)
        put_back(2)
        put_back(3)
        for t in range(PACK):
            weigh(t)

        z_codes = keep.tile([P, S], U32, name="z_codes", align_bytes=MX_ALIGN)
        z_plane = keep.tile([P, S], U8, name="z_plane", align_bytes=MX_ALIGN)
        for u in range(2):
            cols = slice(W * u, W * (u + 1))
            nc.vector.quantize_mx(
                z_codes[:, cols].bitcast(FP8X4), z_plane[:, cols], z_bf[u][:].rearrange("p c t -> p (c t)")
            )

        def product(bank, m, cols):
            rows = slice(P * (m % 2), P * (m % 2 + 1))
            nc.tensor.matmul_mx(
                bank[:], lhsT=d_codes[m // 2][:, rows].bitcast(FP8X4), lhsT_scale=d_plane[:, P * m : P * (m + 1)],
                rhs=z_codes[:, cols].bitcast(FP8X4), rhs_scale=z_plane[:, cols], start=True, stop=True,
            )

        def finish(m, ds2, ds3):
            res = keep.tile([P, S], F32, name=f"res{m}")
            nc.vector.tensor_tensor(res[:], ds2[:, 0:S], ds3[:, 0:S], MAX)
            nc.sync.dma_start(out[P * m : P * (m + 1), :], res[:])

        ds2 = keep.tile([P, S], F32, name="ds2_0")
        ds3 = keep.tile([P, S], F32, name="ds3_0")
        for u in range(2):
            bank = psum.tile([P, W], F32, name=f"h_bank0_{u}")
            product(bank, 0, slice(W * u, W * (u + 1)))
            h = keep.tile([P, W], F32, name=f"h0_{u}")
            if u == 0:
                nc.scalar.activation(h[:], bank[:], COPY, scale=H_SCALE)
            else:
                nc.vector.tensor_scalar(h[:], bank[:], H_SCALE, None, MULT)
            entries = slice(W // GROUP * u, W // GROUP * (u + 1))
            nc.scalar.activation(ds2[:].indirect(n3_l[:, entries]), h[:], COPY)
            nc.scalar.activation(ds3[:].indirect(n4_l[:, entries]), h[:], COPY)
        pick_d_words(1, "z_bf1")
        finish(0, ds2, ds3)

        for m in range(1, PACK):
            bank = psum.tile([P, S], F32, name=f"h_bank{m}")
            product(bank, m, slice(0, S))
            h = keep.tile([P, S], F32, name=f"h{m}")
            nc.vector.tensor_scalar(h[:], bank[:], H_SCALE, None, MULT)
            ds2 = keep.tile([P, 2 * S], F32, name=f"ds2_{m}")
            ds3 = keep.tile([P, 2 * S], F32, name=f"ds3_{m}")
            nc.scalar.activation(ds2[:].indirect(n3_l[:]), h[:], COPY)
            nc.scalar.activation(ds3[:].indirect(n4_l[:]), h[:], COPY)
            finish(m, ds2, ds3)
